import numpy as np
import ml_dtypes


def mxq(x, axis, fmt="e4m3"):
    dtype, down = {"e4m3": (ml_dtypes.float8_e4m3fn, 7), "e5m2": (ml_dtypes.float8_e5m2, 14)}[fmt]
    v = np.moveaxis(np.asarray(x, np.float32).astype(ml_dtypes.bfloat16).astype(np.float64), axis, -1)
    blocks = v.reshape(v.shape[:-1] + (-1, 32))
    amax = np.abs(blocks).max(-1, keepdims=True)
    byte = np.maximum(np.where(amax > 0, np.frexp(amax)[1] - 1 + 127, 0) - down, 1)
    scale = np.exp2(byte - 127.0)
    codes = (blocks / scale).astype(np.float32).astype(dtype).astype(np.float64)
    return np.moveaxis((codes * scale).reshape(v.shape), -1, axis)


WIDE = False


def mx_kscale(k):
    if not WIDE:
        return np.ones(k)
    levels = np.array([10, -10, 5, -5, 0])
    if k % 512:
        return np.exp2(np.random.permutation(np.resize(levels, k // 32))).repeat(32)
    a = np.empty((k // 512, 16))
    for p in range(k // 512):
        a[p, :8] = np.random.permutation(np.resize(levels, 8))
        for g in range(8):
            far = levels[np.abs(levels - a[p, g]) >= 10]
            a[p, g + 8] = far[np.random.randint(len(far))]
    return np.exp2(a.ravel()).repeat(32)


def f64(x):
    return np.asarray(x).astype(np.float64)


def striped(idx):
    return np.tile(idx.reshape(-1, 16).T, (8, 1)).astype(np.uint16)


def unstriped(offs):
    return offs[:16].T.reshape(-1).astype(np.int64)


def striped8(idx):
    return np.concatenate([x.reshape(-1, 16).T for x in idx]).astype(np.uint16)


def runs(offs, k):
    lists = np.stack([offs[16 * r : 16 * r + 16].T.reshape(-1) for r in range(8)]).astype(np.int64)
    return lists[np.arange(k) % 512 // 64]


def pack_weight(w):
    k, n = w.shape
    w = f64(np.asarray(w, np.float32).astype(ml_dtypes.bfloat16)).reshape(k // 32, 32, n)
    amax = np.abs(w).max(1)
    byte = np.clip(np.where(amax > 0, np.frexp(amax)[1] - 1 + 127 - 7, 1), 1, 254)
    scaled = (w * np.exp2(127.0 - byte)[:, None, :]).reshape(k, n).astype(np.float32)
    words = np.ascontiguousarray(scaled.reshape(k // 512, 128, 4, n).transpose(0, 1, 3, 2)).astype(ml_dtypes.float8_e4m3fn).view(np.uint8)
    return words, np.ascontiguousarray(byte.astype(np.uint8).reshape(k // 512, 16, n))


def unpack_weight(words, scales):
    g, p, n, _ = words.shape
    vals = np.ascontiguousarray(words).view(ml_dtypes.float8_e4m3fn).astype(np.float64) * np.repeat(np.exp2(scales.astype(np.float64) - 127.0), 8, axis=1)[..., None]
    return vals.transpose(0, 1, 3, 2).reshape(g * 512, n)


K, T, S, V, N, H = 512, 1024, 512, 256, 512, 512


def setup_inputs():
    n = np.random.standard_normal
    s = mx_kscale(K)[:, None]
    u = mx_kscale(H)
    packed_xT = pack_weight(n((K, T)) * s)
    return {
        "x_words": packed_xT[0],
        "x_scales": packed_xT[1],
        "w1": (n((K, H)) / np.sqrt(K) / s * u).astype(np.float32),
        "w2": (n((K, H)) / np.sqrt(K) / s * u).astype(np.float32),
        "w3": (n((H, N)) / np.sqrt(H) / u[:, None]).astype(np.float32),
        "offs": striped(np.random.permutation(T)[:S]),
        "new": striped(np.random.permutation(T)[:V]),
        "at": striped8(np.stack([np.random.permutation(S)[:V] for _ in range(8)])),
    }


def reference(x_words, x_scales, w1, w2, w3, offs, new, at):
    x_new = unpack_weight(x_words, x_scales)[:, unstriped(new)]
    e = mxq(f64(w2), 0, "e4m3").T @ x_new
    xq = unpack_weight(x_words, x_scales)[:, unstriped(offs)]
    y = mxq(f64(w1), 0, "e4m3").T @ xq
    z = y.copy()
    z[np.arange(H)[:, None], runs(at, H)] = e
    return mxq(f64(w3), 0, "e4m3").T @ mxq(z, 0, "e4m3")

@@ -1,0 +1,160 @@
+from contextlib import ExitStack
+
+import concourse.mybir as mybir
+
+K, T, S, V, N, H = 512, 1024, 512, 256, 512, 512
+FLOPS = 2 * K * H * (S + V) + 2 * H * N * S
+
+F32 = mybir.dt.float32
+BF16 = mybir.dt.bfloat16
+I32 = mybir.dt.int32
+U32 = mybir.dt.uint32
+U16 = mybir.dt.uint16
+U8 = mybir.dt.uint8
+FP8X4 = mybir.dt.float8_e4m3fn_x4
+MULT, ADD = mybir.AluOpType.mult, mybir.AluOpType.add
+
+P = 128
+PACK = 4
+PIECES = ((0, 128), (128, 256), (256, 512))
+VECTOR_FROM = 384
+
+
+def tile_picked_splice_none_p_kernel(tc, x_words, x_scales, w1, w2, w3, offs, new, at, out):
+    nc = tc.nc
+    with ExitStack() as ctx:
+        held = ctx.enter_context(tc.tile_pool(name="held", bufs=1))
+        psum = ctx.enter_context(tc.psum_pool(name="psum", bufs=1))
+
+        def sb(name, shape, dtype, tag=None):
+            return held.tile(shape, dtype, name=name, tag=tag or name, align_bytes=64)
+
+        offs_sb = held.tile([P, S // 16], U16, name="offs_sb")
+        new_sb = held.tile([P, V // 16], U16, name="new_sb")
+        at_sb = held.tile([P, V // 16], U16, name="at_sb")
+        words = sb("words", [P, T], I32)
+        scales = sb("scales", [P, T], U8)
+        w1_raw = sb("w1_raw", [P, PACK, H], F32)
+        w2_raw = sb("w2_raw", [P, PACK, H], F32)
+        w3_raw = sb("w3_raw", [P, PACK, N], F32)
+
+        nc.gpsimd.memset(scales[:].bitcast(I32), 0)
+        nc.sync.dma_start(words[:], x_words[0].rearrange("p c r -> p (c r)").bitcast(I32))
+        nc.sync.dma_start(offs_sb[:], offs)
+        nc.sync.dma_start(new_sb[:], new)
+        for q in range(4):
+            nc.sync.dma_start(scales[32 * q : 32 * q + 4, :].bitcast(I32), x_scales[0, 4 * q : 4 * q + 4, :].bitcast(I32))
+        nc.sync.dma_start(w1_raw[:], w1.rearrange("(p j) c -> p j c", j=PACK))
+        nc.sync.dma_start(w2_raw[:], w2.rearrange("(p j) c -> p j c", j=PACK))
+        nc.sync.dma_start(at_sb[:], at)
+        w3_rows = w3.rearrange("(g t u) n -> t g u n", t=PACK, u=4)
+        for t in range(PACK):
+            nc.sync.dma_start(w3_raw[:, t, :], w3_rows[t])
+
+        old_words = sb("old_words", [P, S], U32)
+        old_scales = sb("old_scales", [P, S], U8)
+        new_words = sb("new_words", [P, V], U32)
+        new_scales = sb("new_scales", [P, V], U8)
+        nc.vector.tensor_copy(old_words[:], words[:].bitcast(U32).indirect(offs_sb[:]))
+        nc.vector.tensor_copy(old_scales[:], scales[:].indirect(offs_sb[:]))
+        nc.vector.tensor_copy(new_words[:], words[:].bitcast(U32).indirect(new_sb[:]))
+        nc.vector.tensor_copy(new_scales[:], scales[:].indirect(new_sb[:]))
+
+        def round_plane(copy, raw, t, name, tag=None):
+            grouped = sb(name, [P, P * PACK], BF16, tag)
+            copy(
+                grouped[:].rearrange("p (g u j) -> p g j u", u=4, j=PACK),
+                raw[:].rearrange("p j (g t u) -> p t g j u", t=PACK, u=4)[:, t],
+            )
+            return grouped
+
+        def quantize(grouped, name, tag=None, scale_tag=None):
+            width = grouped[:].shape[1] // PACK
+            codes = sb(name + "_codes", [P, width], U32, tag)
+            code_scales = sb(name + "_scales", [P, width], U8, scale_tag)
+            nc.vector.quantize_mx(out=codes[:].bitcast(FP8X4), scales=code_scales[:], in_=grouped[:])
+            return codes, code_scales
+
+        def product(acc, lhs, rhs):
+            nc.tensor.matmul_mx(
+                out=acc, lhsT=lhs[0].bitcast(FP8X4), lhsT_scale=lhs[1], rhs=rhs[0].bitcast(FP8X4), rhs_scale=rhs[1], start=True, stop=True
+            )
+
+        def gpsimd_round(grouped, raw):
+            nc.gpsimd.tensor_scalar(grouped, raw, 1.0, 0.0, op0=MULT, op1=ADD)
+
+        w1_grouped = [round_plane(nc.scalar.copy if t < 3 else nc.vector.tensor_copy, w1_raw, t, "w1g%d" % t) for t in range(PACK)]
+        w1_q = [quantize(w1_grouped[t], "w1q%d" % t, *(("zg0", "zg1") if t == 3 else ())) for t in range(PACK)]
+        z, e = [], []
+
+        y_accs = []
+
+        def old_product(t, bank):
+            codes, code_scales = w1_q[t]
+            y_acc = psum.tile([P, S], F32, name="y_acc%d" % t, tag=bank)
+            product(y_acc[:], (codes[:], code_scales[:]), (old_words[:], old_scales[:]))
+            y_accs.append(y_acc)
+
+        def old_copy(t):
+            z_t = sb("z%d" % t, [P, S], F32)
+            nc.scalar.copy(z_t[:], y_accs[t][:])
+            z.append(z_t)
+
+        old_product(0, "bank0")
+        old_product(1, "bank1")
+        old_copy(0)
+        w2_grouped = [round_plane(nc.vector.tensor_copy, w2_raw, t, "w2g%d" % t) for t in range(2)]
+        for t in range(PACK):
+            codes, code_scales = quantize(w2_grouped[t], "w2q%d" % t, {0: "z1", 3: "zg2"}.get(t))
+            if t == 0:
+                w2_grouped.append(round_plane(nc.vector.tensor_copy, w2_raw, 2, "w2g2"))
+                w2_grouped.append(round_plane(nc.vector.tensor_copy, w2_raw, 3, "w2g3", "late"))
+            e_acc = psum.tile([P, V], F32, name="e_acc%d" % t, tag="bank%d" % (2 + t))
+            product(e_acc[:], (codes[:], code_scales[:]), (new_words[:], new_scales[:]))
+            e_t = sb("e%d" % t, [P, V], F32)
+            nc.scalar.copy(e_t[:], e_acc[:])
+            e.append(e_t)
+            if t + 2 < PACK:
+                old_product(2 + t, "bank%d" % (2 + t))
+            if t + 1 < PACK:
+                old_copy(1 + t)
+
+        w3_grouped = sb("w3g", [P, N * PACK], BF16, "late")
+        gpsimd_round(w3_grouped[:].rearrange("p (n t) -> p n t", t=PACK), w3_raw[:].rearrange("p t n -> p n t"))
+
+        z_grouped = [sb("zg%d" % i, [P, (hi - lo) * PACK], BF16) for i, (lo, hi) in enumerate(PIECES)]
+
+        def place(copy, t, i, lo, hi, slots=1):
+            first = PIECES[i][0]
+            target = z_grouped[i][:].rearrange("p (c t) -> p c t", t=PACK)[:, lo - first : hi - first, t : t + slots]
+            copy(target, z[t][:, lo:hi].unsqueeze(2).to_broadcast([P, hi - lo, slots]))
+
+        for t in range(PACK):
+            nc.vector.tensor_copy(z[t][:].indirect(at_sb[:]), e[t][:])
+            if t == PACK - 1:
+                w3_codes, w3_scales = quantize(w3_grouped, "w3q")
+            for i, (lo, hi) in enumerate(PIECES):
+                if t < PACK - 2 or hi <= VECTOR_FROM:
+                    place(nc.scalar.copy, t, i, lo, hi)
+                elif t == PACK - 2:
+                    place(nc.scalar.copy, t, i, lo, VECTOR_FROM)
+                    place(nc.scalar.copy, t, i, VECTOR_FROM, hi, slots=2)
+                else:
+                    place(nc.scalar.copy, t, i, lo, VECTOR_FROM)
+                    place(nc.vector.tensor_copy, t, i, VECTOR_FROM, hi)
+
+        bank = 0
+        for i, (lo, hi) in enumerate(PIECES):
+            z_codes, z_scales = quantize(z_grouped[i], "zq%d" % i)
+            width = hi - lo
+            blocks = 256 // width
+            for first in range(0, N // P, blocks):
+                acc = psum.tile([P, blocks, width], F32, name="acc%d" % bank, tag="bank%d" % bank)
+                for a in range(blocks):
+                    cols = slice((first + a) * P, (first + a + 1) * P)
+                    product(acc[:, a, :], (w3_codes[:, cols], w3_scales[:, cols]), (z_codes[:], z_scales[:]))
+                result = sb("result%d" % bank, [P, blocks, width], F32)
+                (nc.scalar.copy if bank % 2 == 0 else nc.vector.tensor_copy)(result[:], acc[:])
+                rows = out[first * P : (first + blocks) * P, lo:hi]
+                nc.sync.dma_start(rows.rearrange("(a p) c -> p a c", p=P), result[:])
+                bank = bank + 1

@@ -12,12 +12,10 @@ U32 = mybir.dt.uint32
 U16 = mybir.dt.uint16
 U8 = mybir.dt.uint8
 FP8X4 = mybir.dt.float8_e4m3fn_x4
-MULT, ADD = mybir.AluOpType.mult, mybir.AluOpType.add
 
 P = 128
 PACK = 4
 PIECES = ((0, 128), (128, 256), (256, 512))
-VECTOR_FROM = 384
 
 
 def tile_picked_splice_none_p_kernel(tc, x_words, x_scales, w1, w2, w3, offs, new, at, out):
@@ -80,11 +78,8 @@ def tile_picked_splice_none_p_kernel(tc, x_words, x_scales, w1, w2, w3, offs, ne
                 out=acc, lhsT=lhs[0].bitcast(FP8X4), lhsT_scale=lhs[1], rhs=rhs[0].bitcast(FP8X4), rhs_scale=rhs[1], start=True, stop=True
             )
 
-        def gpsimd_round(grouped, raw):
-            nc.gpsimd.tensor_scalar(grouped, raw, 1.0, 0.0, op0=MULT, op1=ADD)
-
         w1_grouped = [round_plane(nc.scalar.copy if t < 3 else nc.vector.tensor_copy, w1_raw, t, "w1g%d" % t) for t in range(PACK)]
-        w1_q = [quantize(w1_grouped[t], "w1q%d" % t, *(("zg0", "zg1") if t == 3 else ())) for t in range(PACK)]
+        w1_q = [quantize(w1_grouped[t], "w1q%d" % t, *(("pairs0", "pairs1") if t == 3 else ())) for t in range(PACK)]
         z, e = [], []
 
         y_accs = []
@@ -105,10 +100,10 @@ def tile_picked_splice_none_p_kernel(tc, x_words, x_scales, w1, w2, w3, offs, ne
         old_copy(0)
         w2_grouped = [round_plane(nc.vector.tensor_copy, w2_raw, t, "w2g%d" % t) for t in range(2)]
         for t in range(PACK):
-            codes, code_scales = quantize(w2_grouped[t], "w2q%d" % t, {0: "z1", 3: "zg2"}.get(t))
+            codes, code_scales = quantize(w2_grouped[t], "w2q%d" % t, "pairs2" if t == 3 else None)
             if t == 0:
                 w2_grouped.append(round_plane(nc.vector.tensor_copy, w2_raw, 2, "w2g2"))
-                w2_grouped.append(round_plane(nc.vector.tensor_copy, w2_raw, 3, "w2g3", "late"))
+                w2_grouped.append(round_plane(nc.vector.tensor_copy, w2_raw, 3, "w2g3"))
             e_acc = psum.tile([P, V], F32, name="e_acc%d" % t, tag="bank%d" % (2 + t))
             product(e_acc[:], (codes[:], code_scales[:]), (new_words[:], new_scales[:]))
             e_t = sb("e%d" % t, [P, V], F32)
@@ -119,33 +114,28 @@ def tile_picked_splice_none_p_kernel(tc, x_words, x_scales, w1, w2, w3, offs, ne
             if t + 1 < PACK:
                 old_copy(1 + t)
 
-        w3_grouped = sb("w3g", [P, N * PACK], BF16, "late")
-        gpsimd_round(w3_grouped[:].rearrange("p (n t) -> p n t", t=PACK), w3_raw[:].rearrange("p t n -> p n t"))
+        w3_grouped = sb("w3g", [P, N * PACK], BF16)
+        for first in range(0, N, P):
+            nc.scalar.copy(
+                w3_grouped[:, first * PACK : (first + P) * PACK].rearrange("p (c u t) -> p c t u", u=4, t=PACK),
+                w3_raw[:, :, first : first + P].rearrange("p t (c u) -> p c t u", u=4),
+            )
 
-        z_grouped = [sb("zg%d" % i, [P, (hi - lo) * PACK], BF16) for i, (lo, hi) in enumerate(PIECES)]
-
-        def place(copy, t, i, lo, hi, slots=1):
-            first = PIECES[i][0]
-            target = z_grouped[i][:].rearrange("p (c t) -> p c t", t=PACK)[:, lo - first : hi - first, t : t + slots]
-            copy(target, z[t][:, lo:hi].unsqueeze(2).to_broadcast([P, hi - lo, slots]))
-
+        pairs = [sb("pairs%d" % i, [P, 2, hi - lo, 2], BF16) for i, (lo, hi) in enumerate(PIECES)]
         for t in range(PACK):
             nc.vector.tensor_copy(z[t][:].indirect(at_sb[:]), e[t][:])
-            if t == PACK - 1:
-                w3_codes, w3_scales = quantize(w3_grouped, "w3q")
             for i, (lo, hi) in enumerate(PIECES):
-                if t < PACK - 2 or hi <= VECTOR_FROM:
-                    place(nc.scalar.copy, t, i, lo, hi)
-                elif t == PACK - 2:
-                    place(nc.scalar.copy, t, i, lo, VECTOR_FROM)
-                    place(nc.scalar.copy, t, i, VECTOR_FROM, hi, slots=2)
-                else:
-                    place(nc.scalar.copy, t, i, lo, VECTOR_FROM)
-                    place(nc.vector.tensor_copy, t, i, VECTOR_FROM, hi)
+                nc.scalar.copy(pairs[i][:, t // 2, :, t % 2], z[t][:, lo:hi])
+        w3_codes, w3_scales = quantize(w3_grouped, "w3q")
 
         bank = 0
         for i, (lo, hi) in enumerate(PIECES):
-            z_codes, z_scales = quantize(z_grouped[i], "zq%d" % i)
+            z_grouped = sb("zg%d" % i, [P, (hi - lo) * PACK], BF16)
+            nc.vector.tensor_copy(
+                z_grouped[:].bitcast(F32).rearrange("p (c a) -> p c a", a=2),
+                pairs[i][:].rearrange("p a c b -> p (a c b)").bitcast(F32).rearrange("p (a c) -> p c a", a=2),
+            )
+            z_codes, z_scales = quantize(z_grouped, "zq%d" % i)
             width = hi - lo
             blocks = 256 // width
             for first in range(0, N // P, blocks):

@@ -12,6 +12,7 @@ U32 = mybir.dt.uint32
 U16 = mybir.dt.uint16
 U8 = mybir.dt.uint8
 FP8X4 = mybir.dt.float8_e4m3fn_x4
+MULT, ADD = mybir.AluOpType.mult, mybir.AluOpType.add
 
 P = 128
 PACK = 4
@@ -100,10 +101,10 @@ def tile_picked_splice_none_p_kernel(tc, x_words, x_scales, w1, w2, w3, offs, ne
         old_copy(0)
         w2_grouped = [round_plane(nc.vector.tensor_copy, w2_raw, t, "w2g%d" % t) for t in range(2)]
         for t in range(PACK):
-            codes, code_scales = quantize(w2_grouped[t], "w2q%d" % t, "pairs2" if t == 3 else None)
+            codes, code_scales = quantize(w2_grouped[t], "w2q%d" % t, {1: "z1", 3: "pairs2"}.get(t))
             if t == 0:
                 w2_grouped.append(round_plane(nc.vector.tensor_copy, w2_raw, 2, "w2g2"))
-                w2_grouped.append(round_plane(nc.vector.tensor_copy, w2_raw, 3, "w2g3"))
+                w2_grouped.append(round_plane(nc.scalar.copy, w2_raw, 3, "w2g3", "late"))
             e_acc = psum.tile([P, V], F32, name="e_acc%d" % t, tag="bank%d" % (2 + t))
             product(e_acc[:], (codes[:], code_scales[:]), (new_words[:], new_scales[:]))
             e_t = sb("e%d" % t, [P, V], F32)
@@ -111,15 +112,13 @@ def tile_picked_splice_none_p_kernel(tc, x_words, x_scales, w1, w2, w3, offs, ne
             e.append(e_t)
             if t + 2 < PACK:
                 old_product(2 + t, "bank%d" % (2 + t))
-            if t + 1 < PACK:
-                old_copy(1 + t)
+            if t >= 1:
+                old_copy(t)
 
-        w3_grouped = sb("w3g", [P, N * PACK], BF16)
-        for first in range(0, N, P):
-            nc.scalar.copy(
-                w3_grouped[:, first * PACK : (first + P) * PACK].rearrange("p (c u t) -> p c t u", u=4, t=PACK),
-                w3_raw[:, :, first : first + P].rearrange("p t (c u) -> p c t u", u=4),
-            )
+        w3_grouped = sb("w3g", [P, N * PACK], BF16, "late")
+        nc.gpsimd.tensor_scalar(
+            w3_grouped[:].rearrange("p (n t) -> p n t", t=PACK), w3_raw[:].rearrange("p t n -> p n t"), 1.0, 0.0, op0=MULT, op1=ADD
+        )
 
         pairs = [sb("pairs%d" % i, [P, 2, hi - lo, 2], BF16) for i, (lo, hi) in enumerate(PIECES)]
         for t in range(PACK):
@@ -144,7 +143,7 @@ def tile_picked_splice_none_p_kernel(tc, x_words, x_scales, w1, w2, w3, offs, ne
                     cols = slice((first + a) * P, (first + a + 1) * P)
                     product(acc[:, a, :], (w3_codes[:, cols], w3_scales[:, cols]), (z_codes[:], z_scales[:]))
                 result = sb("result%d" % bank, [P, blocks, width], F32)
-                (nc.scalar.copy if bank % 2 == 0 else nc.vector.tensor_copy)(result[:], acc[:])
+                (nc.vector.tensor_copy if bank in (4, 6) else nc.scalar.copy)(result[:], acc[:])
                 rows = out[first * P : (first + blocks) * P, lo:hi]
                 nc.sync.dma_start(rows.rearrange("(a p) c -> p a c", p=P), result[:])
                 bank = bank + 1

@@ -79,14 +79,13 @@ def tile_picked_splice_none_p_kernel(tc, x_words, x_scales, w1, w2, w3, offs, ne
                 out=acc, lhsT=lhs[0].bitcast(FP8X4), lhsT_scale=lhs[1], rhs=rhs[0].bitcast(FP8X4), rhs_scale=rhs[1], start=True, stop=True
             )
 
-        w1_grouped = [round_plane(nc.scalar.copy if t < 3 else nc.vector.tensor_copy, w1_raw, t, "w1g%d" % t) for t in range(PACK)]
-        w1_q = [quantize(w1_grouped[t], "w1q%d" % t, *(("pairs0", "pairs1") if t == 3 else ())) for t in range(PACK)]
+        w1_grouped = [round_plane(nc.scalar.copy, w1_raw, t, "w1g%d" % t) for t in range(PACK)]
         z, e = [], []
 
         y_accs = []
 
         def old_product(t, bank):
-            codes, code_scales = w1_q[t]
+            codes, code_scales = quantize(w1_grouped[t], "w1q%d" % t, *(("pairs0", "pairs1") if t == 3 else ()))
             y_acc = psum.tile([P, S], F32, name="y_acc%d" % t, tag=bank)
             product(y_acc[:], (codes[:], code_scales[:]), (old_words[:], old_scales[:]))
             y_accs.append(y_acc)

@@ -16,17 +16,25 @@ MULT, ADD = mybir.AluOpType.mult, mybir.AluOpType.add
 
 P = 128
 PACK = 4
-PIECES = ((0, 128), (128, 256), (256, 512))
+ORDER = (1, 3, 0, 2)
+PIECES = ((0, 128), (128, 256), (256, 384), (384, 512))
+VECTOR_BANKS = (0, 1, 4, 6)
 
 
 def tile_picked_splice_none_p_kernel(tc, x_words, x_scales, w1, w2, w3, offs, new, at, out):
     nc = tc.nc
     with ExitStack() as ctx:
         held = ctx.enter_context(tc.tile_pool(name="held", bufs=1))
+        reused = ctx.enter_context(tc.tile_pool(name="reused", bufs=1))
         psum = ctx.enter_context(tc.psum_pool(name="psum", bufs=1))
 
         def sb(name, shape, dtype, tag=None):
+            if isinstance(tag, int):
+                return reused.tile(shape, dtype, name=name, tag=name, align_bytes=64, offset=tag)
             return held.tile(shape, dtype, name=name, tag=tag or name, align_bytes=64)
+
+        def gpsimd_copy(dst, src):
+            nc.gpsimd.tensor_scalar(dst, src, 1.0, 0.0, op0=MULT, op1=ADD)
 
         offs_sb = held.tile([P, S // 16], U16, name="offs_sb")
         new_sb = held.tile([P, V // 16], U16, name="new_sb")
@@ -35,9 +43,9 @@ def tile_picked_splice_none_p_kernel(tc, x_words, x_scales, w1, w2, w3, offs, ne
         scales = sb("scales", [P, T], U8)
         w1_raw = sb("w1_raw", [P, PACK, H], F32)
         w2_raw = sb("w2_raw", [P, PACK, H], F32)
-        w3_raw = sb("w3_raw", [P, PACK, N], F32)
+        w3_raw = sb("w3_raw", [P, PACK, N], F32, 0)
 
-        nc.gpsimd.memset(scales[:].bitcast(I32), 0)
+        nc.vector.memset(scales[:].bitcast(I32), 0)
         nc.sync.dma_start(words[:], x_words[0].rearrange("p c r -> p (c r)").bitcast(I32))
         nc.sync.dma_start(offs_sb[:], offs)
         nc.sync.dma_start(new_sb[:], new)
@@ -61,17 +69,18 @@ def tile_picked_splice_none_p_kernel(tc, x_words, x_scales, w1, w2, w3, offs, ne
 
         def round_plane(copy, raw, t, name, tag=None):
             grouped = sb(name, [P, P * PACK], BF16, tag)
+            walk = "g u j" if copy is gpsimd_copy else "g j u"
             copy(
-                grouped[:].rearrange("p (g u j) -> p g j u", u=4, j=PACK),
-                raw[:].rearrange("p j (g t u) -> p t g j u", t=PACK, u=4)[:, t],
+                grouped[:].rearrange("p (g u j) -> p " + walk, u=4, j=PACK),
+                raw[:].rearrange("p j (g t u) -> p t " + walk, t=PACK, u=4)[:, t],
             )
             return grouped
 
-        def quantize(grouped, name, tag=None, scale_tag=None):
-            width = grouped[:].shape[1] // PACK
+        def quantize(grouped, name, tag=None):
+            width = grouped.shape[1] // PACK
             codes = sb(name + "_codes", [P, width], U32, tag)
-            code_scales = sb(name + "_scales", [P, width], U8, scale_tag)
-            nc.vector.quantize_mx(out=codes[:].bitcast(FP8X4), scales=code_scales[:], in_=grouped[:])
+            code_scales = sb(name + "_scales", [P, width], U8)
+            nc.vector.quantize_mx(out=codes[:].bitcast(FP8X4), scales=code_scales[:], in_=grouped)
             return codes, code_scales
 
         def product(acc, lhs, rhs):
@@ -79,70 +88,95 @@ def tile_picked_splice_none_p_kernel(tc, x_words, x_scales, w1, w2, w3, offs, ne
                 out=acc, lhsT=lhs[0].bitcast(FP8X4), lhsT_scale=lhs[1], rhs=rhs[0].bitcast(FP8X4), rhs_scale=rhs[1], start=True, stop=True
             )
 
-        w1_grouped = [round_plane(nc.scalar.copy, w1_raw, t, "w1g%d" % t) for t in range(PACK)]
-        z, e = [], []
+        a, b, c, d = ORDER
+        w1_grouped = {}
+        for t, copy in ((a, gpsimd_copy), (b, nc.scalar.copy), (c, nc.scalar.copy), (d, gpsimd_copy)):
+            w1_grouped[t] = round_plane(copy, w1_raw, t, "w1g%d" % t)
+        w1_q = {t: quantize(w1_grouped[t][:], "w1q%d" % t, {c: 9216, d: 8192}.get(t)) for t in ORDER}
 
-        y_accs = []
+        y_acc, z, e = {}, {}, {}
 
         def old_product(t, bank):
-            codes, code_scales = quantize(w1_grouped[t], "w1q%d" % t, *(("pairs0", "pairs1") if t == 3 else ()))
-            y_acc = psum.tile([P, S], F32, name="y_acc%d" % t, tag=bank)
-            product(y_acc[:], (codes[:], code_scales[:]), (old_words[:], old_scales[:]))
-            y_accs.append(y_acc)
+            y_acc[t] = psum.tile([P, S], F32, name="y_acc%d" % t, tag=bank)
+            product(y_acc[t][:], (w1_q[t][0][:], w1_q[t][1][:]), (old_words[:], old_scales[:]))
 
-        def old_copy(t):
-            z_t = sb("z%d" % t, [P, S], F32)
-            nc.scalar.copy(z_t[:], y_accs[t][:])
-            z.append(z_t)
+        def old_copy(t, width, tag=None):
+            z[t] = sb("z%d" % t, [P, width], F32, tag)
+            nc.scalar.copy(z[t][:, :S], y_acc[t][:])
 
-        old_product(0, "bank0")
-        old_product(1, "bank1")
-        old_copy(0)
-        w2_grouped = [round_plane(nc.vector.tensor_copy, w2_raw, t, "w2g%d" % t) for t in range(2)]
-        for t in range(PACK):
-            codes, code_scales = quantize(w2_grouped[t], "w2q%d" % t, {1: "z1", 3: "pairs2"}.get(t))
-            if t == 0:
-                w2_grouped.append(round_plane(nc.vector.tensor_copy, w2_raw, 2, "w2g2"))
-                w2_grouped.append(round_plane(nc.scalar.copy, w2_raw, 3, "w2g3", "late"))
-            e_acc = psum.tile([P, V], F32, name="e_acc%d" % t, tag="bank%d" % (2 + t))
-            product(e_acc[:], (codes[:], code_scales[:]), (new_words[:], new_scales[:]))
-            e_t = sb("e%d" % t, [P, V], F32)
-            nc.scalar.copy(e_t[:], e_acc[:])
-            e.append(e_t)
-            if t + 2 < PACK:
-                old_product(2 + t, "bank%d" % (2 + t))
-            if t >= 1:
-                old_copy(t)
+        def new_product(t, acc, tag=None):
+            codes, code_scales = quantize(w2_grouped[t][:], "w2q%d" % t, tag)
+            product(acc, (codes[:], code_scales[:]), (new_words[:], new_scales[:]))
 
-        w3_grouped = sb("w3g", [P, N * PACK], BF16, "late")
-        nc.gpsimd.tensor_scalar(
-            w3_grouped[:].rearrange("p (n t) -> p n t", t=PACK), w3_raw[:].rearrange("p t n -> p n t"), 1.0, 0.0, op0=MULT, op1=ADD
-        )
+        def new_copy(planes, acc, tag=None):
+            values = sb("e%d" % planes[0], [P, len(planes), V], F32, tag)
+            nc.scalar.copy(values[:], acc[:])
+            for i, t in enumerate(planes):
+                e[t] = values[:, i, :]
 
-        pairs = [sb("pairs%d" % i, [P, 2, hi - lo, 2], BF16) for i, (lo, hi) in enumerate(PIECES)]
-        for t in range(PACK):
-            nc.vector.tensor_copy(z[t][:].indirect(at_sb[:]), e[t][:])
-            for i, (lo, hi) in enumerate(PIECES):
-                nc.scalar.copy(pairs[i][:, t // 2, :, t % 2], z[t][:, lo:hi])
-        w3_codes, w3_scales = quantize(w3_grouped, "w3q")
+        def scatter(t):
+            nc.vector.tensor_copy(z[t][:].indirect(at_sb[:]), e[t])
 
+        old_product(a, "bank0")
+        old_product(b, "bank1")
+        old_copy(a, S)
+        w2_grouped = {t: round_plane(nc.vector.tensor_copy, w2_raw, t, "w2g%d" % t, tag) for t, tag in ((a, "w3g"), (b, None))}
+        w2_grouped[c] = round_plane(nc.scalar.copy, w2_raw, c, "w2g%d" % c)
+        e_acc_a = psum.tile([P, 1, V], F32, name="e_acc_a", tag="bank2")
+        e_acc_b = psum.tile([P, 1, V], F32, name="e_acc_b", tag="bank3")
+        e_acc_cd = psum.tile([P, 2, V], F32, name="e_acc_cd", tag="bank4")
+        new_product(a, e_acc_a[:, 0, :])
+        new_copy((a,), e_acc_a)
+        new_product(b, e_acc_b[:, 0, :], "zb")
+        w2_grouped[d] = round_plane(nc.vector.tensor_copy, w2_raw, d, "w2g%d" % d, "w3g")
+        new_product(c, e_acc_cd[:, 0, :])
+        new_product(d, e_acc_cd[:, 1, :])
+        old_copy(b, S, "zb")
+        new_copy((b,), e_acc_b)
+        new_copy((c, d), e_acc_cd)
+        old_product(c, "bank3")
+        old_copy(c, 2 * S, 9216)
+        old_product(d, "bank3")
+
+        w3_grouped = sb("w3g", [P, N * PACK], BF16)
+        gpsimd_copy(w3_grouped[:].rearrange("p (n t) -> p n t", t=PACK), w3_raw[:].rearrange("p t n -> p n t"))
+
+        scatter(a)
+        nc.scalar.copy(z[c][:, S:], z[a][:])
+        old_copy(d, 2 * S, 4608)
+        scatter(b)
+        nc.scalar.copy(z[d][:, S:], z[b][:])
+        scatter(c)
+
+        z_grouped = [sb("zg%d" % i, [P, (hi - lo) * PACK], BF16, 8 * lo) for i, (lo, hi) in enumerate(PIECES)]
+
+        def round_pair(copy, t, i):
+            lo, hi = PIECES[i]
+            copy(
+                z_grouped[i][:].rearrange("p (n t) -> p n t", t=PACK)[:, :, t : t + 2],
+                z[t][:].rearrange("p (s n) -> p n s", s=2)[:, lo:hi, :],
+            )
+
+        for i, copy in enumerate((nc.scalar.copy, gpsimd_copy, nc.scalar.copy, gpsimd_copy)):
+            round_pair(copy, c, i)
+        scatter(d)
+        w3_codes, w3_scales = quantize(w3_grouped[:], "w3q", 9216)
+        for i in range(len(PIECES)):
+            round_pair(nc.scalar.copy, d, i)
+
+        banks = (5, 6, 7, 0, 1, 2, 4, 3)
         bank = 0
         for i, (lo, hi) in enumerate(PIECES):
-            z_grouped = sb("zg%d" % i, [P, (hi - lo) * PACK], BF16)
-            nc.vector.tensor_copy(
-                z_grouped[:].bitcast(F32).rearrange("p (c a) -> p c a", a=2),
-                pairs[i][:].rearrange("p a c b -> p (a c b)").bitcast(F32).rearrange("p (a c) -> p c a", a=2),
-            )
-            z_codes, z_scales = quantize(z_grouped, "zq%d" % i)
+            z_codes, z_scales = quantize(z_grouped[i][:], "zq%d" % i)
             width = hi - lo
             blocks = 256 // width
             for first in range(0, N // P, blocks):
-                acc = psum.tile([P, blocks, width], F32, name="acc%d" % bank, tag="bank%d" % bank)
-                for a in range(blocks):
-                    cols = slice((first + a) * P, (first + a + 1) * P)
-                    product(acc[:, a, :], (w3_codes[:, cols], w3_scales[:, cols]), (z_codes[:], z_scales[:]))
+                acc = psum.tile([P, blocks, width], F32, name="acc%d" % bank, tag="bank%d" % banks[bank])
+                for m in range(blocks):
+                    cols = slice((first + m) * P, (first + m + 1) * P)
+                    product(acc[:, m, :], (w3_codes[:, cols], w3_scales[:, cols]), (z_codes[:], z_scales[:]))
                 result = sb("result%d" % bank, [P, blocks, width], F32)
-                (nc.vector.tensor_copy if bank in (4, 6) else nc.scalar.copy)(result[:], acc[:])
+                (nc.vector.tensor_copy if bank in VECTOR_BANKS else nc.scalar.copy)(result[:], acc[:])
                 rows = out[first * P : (first + blocks) * P, lo:hi]
-                nc.sync.dma_start(rows.rearrange("(a p) c -> p a c", p=P), result[:])
+                nc.sync.dma_start(rows.rearrange("(m p) n -> p m n", p=P), result[:])
                 bank = bank + 1

@@ -18,7 +18,6 @@ P = 128
 PACK = 4
 ORDER = (1, 3, 0, 2)
 PIECES = ((0, 128), (128, 256), (256, 384), (384, 512))
-VECTOR_BANKS = (0, 1, 4, 6)
 
 
 def tile_picked_splice_none_p_kernel(tc, x_words, x_scales, w1, w2, w3, offs, new, at, out):
@@ -164,19 +163,28 @@ def tile_picked_splice_none_p_kernel(tc, x_words, x_scales, w1, w2, w3, offs, ne
         for i in range(len(PIECES)):
             round_pair(nc.scalar.copy, d, i)
 
-        banks = (5, 6, 7, 0, 1, 2, 4, 3)
-        bank = 0
-        for i, (lo, hi) in enumerate(PIECES):
+        stores = (
+            ((0, 2), (0, 1), "bank5", nc.vector.tensor_copy),
+            ((0, 2), (1, 2), "bank6", nc.vector.tensor_copy),
+            ((2, 4), (0, 2), "bank7", nc.scalar.copy),
+            ((0, 1), (2, 4), "bank0", nc.vector.tensor_copy),
+            ((1, 2), (2, 4), "bank1", nc.scalar.copy),
+            ((2, 3), (2, 4), "bank2", nc.vector.tensor_copy),
+            ((3, 4), (2, 4), "bank4", nc.scalar.copy),
+        )
+        accs = [
+            psum.tile([P, m1 - m0, (i1 - i0) * P], F32, name="acc%d" % n, tag=bank)
+            for n, ((m0, m1), (i0, i1), bank, copy) in enumerate(stores)
+        ]
+        for i in range(len(PIECES)):
             z_codes, z_scales = quantize(z_grouped[i][:], "zq%d" % i)
-            width = hi - lo
-            blocks = 256 // width
-            for first in range(0, N // P, blocks):
-                acc = psum.tile([P, blocks, width], F32, name="acc%d" % bank, tag="bank%d" % banks[bank])
-                for m in range(blocks):
-                    cols = slice((first + m) * P, (first + m + 1) * P)
-                    product(acc[:, m, :], (w3_codes[:, cols], w3_scales[:, cols]), (z_codes[:], z_scales[:]))
-                result = sb("result%d" % bank, [P, blocks, width], F32)
-                (nc.vector.tensor_copy if bank in VECTOR_BANKS else nc.scalar.copy)(result[:], acc[:])
-                rows = out[first * P : (first + blocks) * P, lo:hi]
-                nc.sync.dma_start(rows.rearrange("(m p) n -> p m n", p=P), result[:])
-                bank = bank + 1
+            for n, ((m0, m1), (i0, i1), bank, copy) in enumerate(stores):
+                if i0 <= i < i1:
+                    for m in range(m0, m1):
+                        cols = slice(m * P, (m + 1) * P)
+                        product(accs[n][:, m - m0, (i - i0) * P : (i - i0 + 1) * P], (w3_codes[:, cols], w3_scales[:, cols]), (z_codes[:], z_scales[:]))
+                if i == i1 - 1:
+                    result = sb("result%d" % n, [P, m1 - m0, (i1 - i0) * P], F32)
+                    copy(result[:], accs[n][:])
+                    rows = out[m0 * P : m1 * P, i0 * P : i1 * P]
+                    nc.sync.dma_start(rows.rearrange("(m p) n -> p m n", p=P), result[:])

@@ -51,7 +51,8 @@ def tile_picked_splice_none_p_kernel(tc, x_words, x_scales, w1, w2, w3, offs, ne
         for q in range(4):
             nc.sync.dma_start(scales[32 * q : 32 * q + 4, :].bitcast(I32), x_scales[0, 4 * q : 4 * q + 4, :].bitcast(I32))
         nc.sync.dma_start(w1_raw[:], w1.rearrange("(p j) c -> p j c", j=PACK))
-        nc.sync.dma_start(w2_raw[:], w2.rearrange("(p j) c -> p j c", j=PACK))
+        for j in (0, 2):
+            nc.sync.dma_start(w2_raw[:, j : j + 2, :], w2.rearrange("(p j) c -> p j c", j=PACK)[:, j : j + 2, :])
         nc.sync.dma_start(at_sb[:], at)
         w3_rows = w3.rearrange("(g t u) n -> t g u n", t=PACK, u=4)
         for t in range(PACK):
@@ -74,6 +75,12 @@ def tile_picked_splice_none_p_kernel(tc, x_words, x_scales, w1, w2, w3, offs, ne
                 raw[:].rearrange("p j (g t u) -> p t " + walk, t=PACK, u=4)[:, t],
             )
             return grouped
+
+        def round_rows(copy, raw, t, grouped, j):
+            copy(
+                grouped[:].rearrange("p (g u j) -> p g j u", u=4, j=PACK)[:, :, j : j + 2, :],
+                raw[:].rearrange("p j (g t u) -> p t g j u", t=PACK, u=4)[:, t, :, j : j + 2, :],
+            )
 
         def quantize(grouped, name, tag=None):
             width = grouped.shape[1] // PACK
@@ -118,8 +125,12 @@ def tile_picked_splice_none_p_kernel(tc, x_words, x_scales, w1, w2, w3, offs, ne
 
         old_product(a, "bank0")
         old_product(b, "bank1")
+        w2_grouped = {t: sb("w2g%d" % t, [P, P * PACK], BF16, tag) for t, tag in ((a, "w3g"), (b, None))}
+        for t in (a, b):
+            round_rows(nc.scalar.copy, w2_raw, t, w2_grouped[t], 0)
         old_copy(a, S)
-        w2_grouped = {t: round_plane(nc.vector.tensor_copy, w2_raw, t, "w2g%d" % t, tag) for t, tag in ((a, "w3g"), (b, None))}
+        for t in (a, b):
+            round_rows(nc.vector.tensor_copy, w2_raw, t, w2_grouped[t], 2)
         w2_grouped[c] = round_plane(nc.scalar.copy, w2_raw, c, "w2g%d" % c)
         e_acc_a = psum.tile([P, 1, V], F32, name="e_acc_a", tag="bank2")
         e_acc_b = psum.tile([P, 1, V], F32, name="e_acc_b", tag="bank3")
@@ -147,21 +158,20 @@ def tile_picked_splice_none_p_kernel(tc, x_words, x_scales, w1, w2, w3, offs, ne
         nc.scalar.copy(z[d][:, S:], z[b][:])
         scatter(c)
 
-        z_grouped = [sb("zg%d" % i, [P, (hi - lo) * PACK], BF16, 8 * lo) for i, (lo, hi) in enumerate(PIECES)]
+        z_grouped = sb("zg", [P, S * PACK], BF16, 0)
 
-        def round_pair(copy, t, i):
-            lo, hi = PIECES[i]
+        def round_pair(copy, t, lo, hi):
             copy(
-                z_grouped[i][:].rearrange("p (n t) -> p n t", t=PACK)[:, :, t : t + 2],
+                z_grouped[:].rearrange("p (n t) -> p n t", t=PACK)[:, lo:hi, t : t + 2],
                 z[t][:].rearrange("p (s n) -> p n s", s=2)[:, lo:hi, :],
             )
 
-        for i, copy in enumerate((nc.scalar.copy, gpsimd_copy, nc.scalar.copy, gpsimd_copy)):
-            round_pair(copy, c, i)
+        round_pair(nc.scalar.copy, c, 0, 3 * P)
+        round_pair(gpsimd_copy, c, 3 * P, S)
         scatter(d)
         w3_codes, w3_scales = quantize(w3_grouped[:], "w3q", 9216)
-        for i in range(len(PIECES)):
-            round_pair(nc.scalar.copy, d, i)
+        for lo, hi in PIECES:
+            round_pair(nc.scalar.copy, d, lo, hi)
 
         stores = (
             ((0, 2), (0, 1), "bank5", nc.vector.tensor_copy),
@@ -176,8 +186,8 @@ def tile_picked_splice_none_p_kernel(tc, x_words, x_scales, w1, w2, w3, offs, ne
             psum.tile([P, m1 - m0, (i1 - i0) * P], F32, name="acc%d" % n, tag=bank)
             for n, ((m0, m1), (i0, i1), bank, copy) in enumerate(stores)
         ]
-        for i in range(len(PIECES)):
-            z_codes, z_scales = quantize(z_grouped[i][:], "zq%d" % i)
+        for i, (lo, hi) in enumerate(PIECES):
+            z_codes, z_scales = quantize(z_grouped[:, lo * PACK : hi * PACK], "zq%d" % i)
             for n, ((m0, m1), (i0, i1), bank, copy) in enumerate(stores):
                 if i0 <= i < i1:
                     for m in range(m0, m1):

@@ -48,8 +48,8 @@ def tile_picked_splice_none_p_kernel(tc, x_words, x_scales, w1, w2, w3, offs, ne
         nc.sync.dma_start(words[:], x_words[0].rearrange("p c r -> p (c r)").bitcast(I32))
         nc.sync.dma_start(offs_sb[:], offs)
         nc.sync.dma_start(new_sb[:], new)
-        for q in range(4):
-            nc.sync.dma_start(scales[32 * q : 32 * q + 4, :].bitcast(I32), x_scales[0, 4 * q : 4 * q + 4, :].bitcast(I32))
+        for r in range(4):
+            nc.sync.dma_start(scales[r:P:32, :].bitcast(I32), x_scales[0, r:16:4, :].bitcast(I32))
         nc.sync.dma_start(w1_raw[:], w1.rearrange("(p j) c -> p j c", j=PACK))
         for j in (0, 2):
             nc.sync.dma_start(w2_raw[:, j : j + 2, :], w2.rearrange("(p j) c -> p j c", j=PACK)[:, j : j + 2, :])

@@ -128,15 +128,19 @@ def tile_picked_splice_none_p_kernel(tc, x_words, x_scales, w1, w2, w3, offs, ne
         w2_grouped = {t: sb("w2g%d" % t, [P, P * PACK], BF16, tag) for t, tag in ((a, "w3g"), (b, None))}
         for t in (a, b):
             round_rows(nc.scalar.copy, w2_raw, t, w2_grouped[t], 0)
-        old_copy(a, S)
         for t in (a, b):
             round_rows(nc.vector.tensor_copy, w2_raw, t, w2_grouped[t], 2)
         w2_grouped[c] = round_plane(nc.scalar.copy, w2_raw, c, "w2g%d" % c)
-        e_acc_a = psum.tile([P, 1, V], F32, name="e_acc_a", tag="bank2")
+        old_copy(a, S, "w1g%d" % d)
         e_acc_b = psum.tile([P, 1, V], F32, name="e_acc_b", tag="bank3")
         e_acc_cd = psum.tile([P, 2, V], F32, name="e_acc_cd", tag="bank4")
-        new_product(a, e_acc_a[:, 0, :])
-        new_copy((a,), e_acc_a)
+        codes, code_scales = quantize(w2_grouped[a][:], "w2q%d" % a)
+        e_first = sb("e%d" % a, [P, V], F32)
+        for lo, bank in ((0, "bank2"), (P, "bank5")):
+            acc = psum.tile([P, P], F32, name="e_acc_a%d" % lo, tag=bank)
+            product(acc[:], (codes[:], code_scales[:]), (new_words[:, lo : lo + P], new_scales[:, lo : lo + P]))
+            nc.scalar.copy(e_first[:, lo : lo + P], acc[:])
+        e[a] = e_first[:]
         new_product(b, e_acc_b[:, 0, :], "zb")
         w2_grouped[d] = round_plane(nc.vector.tensor_copy, w2_raw, d, "w2g%d" % d, "w3g")
         new_product(c, e_acc_cd[:, 0, :])

@@ -177,28 +177,38 @@ def tile_picked_splice_none_p_kernel(tc, x_words, x_scales, w1, w2, w3, offs, ne
         for lo, hi in PIECES:
             round_pair(nc.scalar.copy, d, lo, hi)
 
+        z_codes = sb("z_codes", [P, S], U32)
+        z_scales = sb("z_scales", [P, S], U8)
+        for lo, hi in PIECES:
+            nc.vector.quantize_mx(out=z_codes[:, lo:hi].bitcast(FP8X4), scales=z_scales[:, lo:hi], in_=z_grouped[:, lo * PACK : hi * PACK])
+
         stores = (
-            ((0, 2), (0, 1), "bank5", nc.vector.tensor_copy),
-            ((0, 2), (1, 2), "bank6", nc.vector.tensor_copy),
-            ((2, 4), (0, 2), "bank7", nc.scalar.copy),
-            ((0, 1), (2, 4), "bank0", nc.vector.tensor_copy),
-            ((1, 2), (2, 4), "bank1", nc.scalar.copy),
-            ((2, 3), (2, 4), "bank2", nc.vector.tensor_copy),
-            ((3, 4), (2, 4), "bank4", nc.scalar.copy),
+            (0, (0, P), "bank6", nc.vector.tensor_copy),
+            (1, (0, 2 * P), "bank7", nc.vector.tensor_copy),
+            (2, (0, 2 * P), "bank0", nc.scalar.copy),
+            (3, (0, 2 * P), "bank1", nc.vector.tensor_copy),
+            (0, (P, S), "bank2", nc.scalar.copy),
+            (1, (2 * P, S), "bank5", nc.vector.tensor_copy),
+            (2, (2 * P, S), "bank3", nc.scalar.copy),
+            (3, (2 * P, S), "bank4", nc.vector.tensor_copy),
         )
-        accs = [
-            psum.tile([P, m1 - m0, (i1 - i0) * P], F32, name="acc%d" % n, tag=bank)
-            for n, ((m0, m1), (i0, i1), bank, copy) in enumerate(stores)
-        ]
-        for i, (lo, hi) in enumerate(PIECES):
-            z_codes, z_scales = quantize(z_grouped[:, lo * PACK : hi * PACK], "zq%d" % i)
-            for n, ((m0, m1), (i0, i1), bank, copy) in enumerate(stores):
-                if i0 <= i < i1:
-                    for m in range(m0, m1):
-                        cols = slice(m * P, (m + 1) * P)
-                        product(accs[n][:, m - m0, (i - i0) * P : (i - i0 + 1) * P], (w3_codes[:, cols], w3_scales[:, cols]), (z_codes[:], z_scales[:]))
-                if i == i1 - 1:
-                    result = sb("result%d" % n, [P, m1 - m0, (i1 - i0) * P], F32)
-                    copy(result[:], accs[n][:])
-                    rows = out[m0 * P : m1 * P, i0 * P : i1 * P]
-                    nc.sync.dma_start(rows.rearrange("(m p) n -> p m n", p=P), result[:])
+        accs = [psum.tile([P, hi - lo], F32, name="acc%d" % n, tag=bank) for n, (m, (lo, hi), bank, copy) in enumerate(stores)]
+
+        def last_product(n, lo, hi):
+            m, (first, last), bank, copy = stores[n]
+            rows = slice(m * P, (m + 1) * P)
+            product(accs[n][:, lo - first : hi - first], (w3_codes[:, rows], w3_scales[:, rows]), (z_codes[:, lo:hi], z_scales[:, lo:hi]))
+            if hi == last:
+                result = sb("result%d" % n, [P, last - first], F32)
+                copy(result[:], accs[n][:])
+                nc.sync.dma_start(out[rows, first:last], result[:])
+
+        for n in (0, 1, 2):
+            last_product(n, 0, P)
+        for n in (1, 2):
+            last_product(n, P, 2 * P)
+        last_product(3, 0, 2 * P)
+        for i in (1, 2, 3):
+            last_product(4, i * P, (i + 1) * P)
+        for n in (5, 6, 7):
+            last_product(n, 2 * P, S)

@@ -182,33 +182,38 @@ def tile_picked_splice_none_p_kernel(tc, x_words, x_scales, w1, w2, w3, offs, ne
         for lo, hi in PIECES:
             nc.vector.quantize_mx(out=z_codes[:, lo:hi].bitcast(FP8X4), scales=z_scales[:, lo:hi], in_=z_grouped[:, lo * PACK : hi * PACK])
 
-        stores = (
-            (0, (0, P), "bank6", nc.vector.tensor_copy),
-            (1, (0, 2 * P), "bank7", nc.vector.tensor_copy),
-            (2, (0, 2 * P), "bank0", nc.scalar.copy),
-            (3, (0, 2 * P), "bank1", nc.vector.tensor_copy),
-            (0, (P, S), "bank2", nc.scalar.copy),
-            (1, (2 * P, S), "bank5", nc.vector.tensor_copy),
-            (2, (2 * P, S), "bank3", nc.scalar.copy),
-            (3, (2 * P, S), "bank4", nc.vector.tensor_copy),
-        )
-        accs = [psum.tile([P, hi - lo], F32, name="acc%d" % n, tag=bank) for n, (m, (lo, hi), bank, copy) in enumerate(stores)]
+        stores = ((0, 0, P), (1, 0, 2 * P), (2, 0, 2 * P), (3, 0, 2 * P), (0, P, S), (1, 2 * P, S), (2, 2 * P, S), (3, 2 * P, S))
+        results = [sb("result%d" % n, [P, hi - lo], F32) for n, (m, lo, hi) in enumerate(stores)]
 
-        def last_product(n, lo, hi):
-            m, (first, last), bank, copy = stores[n]
+        def last_product(m, acc, lo, hi):
             rows = slice(m * P, (m + 1) * P)
-            product(accs[n][:, lo - first : hi - first], (w3_codes[:, rows], w3_scales[:, rows]), (z_codes[:, lo:hi], z_scales[:, lo:hi]))
-            if hi == last:
-                result = sb("result%d" % n, [P, last - first], F32)
-                copy(result[:], accs[n][:])
-                nc.sync.dma_start(out[rows, first:last], result[:])
+            product(acc, (w3_codes[:, rows], w3_scales[:, rows]), (z_codes[:, lo:hi], z_scales[:, lo:hi]))
 
-        for n in (0, 1, 2):
-            last_product(n, 0, P)
-        for n in (1, 2):
-            last_product(n, P, 2 * P)
-        last_product(3, 0, 2 * P)
-        for i in (1, 2, 3):
-            last_product(4, i * P, (i + 1) * P)
-        for n in (5, 6, 7):
-            last_product(n, 2 * P, S)
+        def empty(n, acc, lo, hi, copy):
+            m, first, last = stores[n]
+            copy(results[n][:, lo - first : hi - first], acc[:])
+            if hi == last:
+                nc.sync.dma_start(out[m * P : (m + 1) * P, first:last], results[n][:])
+
+        def lone(n, lo, hi, bank, copy):
+            acc = psum.tile([P, hi - lo], F32, name="acc%d_%d" % (n, lo), tag=bank)
+            last_product(stores[n][0], acc[:], lo, hi)
+            empty(n, acc, lo, hi, copy)
+
+        lone(0, 0, P, "bank6", nc.scalar.copy)
+        acc_1 = psum.tile([P, 2 * P], F32, name="acc_1", tag="bank7")
+        acc_2 = psum.tile([P, 2 * P], F32, name="acc_2", tag="bank0")
+        for lo in (0, P):
+            last_product(1, acc_1[:, lo : lo + P], lo, lo + P)
+            last_product(2, acc_2[:, lo : lo + P], lo, lo + P)
+        empty(1, acc_1, 0, 2 * P, nc.scalar.copy)
+        empty(2, acc_2, 0, 2 * P, nc.vector.tensor_copy)
+        lone(3, 0, 2 * P, "bank1", nc.scalar.copy)
+        acc_4 = psum.tile([P, 2 * P], F32, name="acc_4", tag="bank2")
+        last_product(0, acc_4[:, :P], P, 2 * P)
+        last_product(0, acc_4[:, P:], 2 * P, 3 * P)
+        empty(4, acc_4, P, 3 * P, nc.vector.tensor_copy)
+        lone(4, 3 * P, S, "bank5", nc.scalar.copy)
+        lone(5, 2 * P, S, "bank3", nc.vector.tensor_copy)
+        lone(6, 2 * P, S, "bank4", nc.scalar.copy)
+        lone(7, 2 * P, S, "bank6", nc.vector.tensor_copy)

@@ -213,7 +213,8 @@ def tile_picked_splice_none_p_kernel(tc, x_words, x_scales, w1, w2, w3, offs, ne
         last_product(0, acc_4[:, :P], P, 2 * P)
         last_product(0, acc_4[:, P:], 2 * P, 3 * P)
         empty(4, acc_4, P, 3 * P, nc.vector.tensor_copy)
-        lone(4, 3 * P, S, "bank5", nc.scalar.copy)
-        lone(5, 2 * P, S, "bank3", nc.vector.tensor_copy)
-        lone(6, 2 * P, S, "bank4", nc.scalar.copy)
-        lone(7, 2 * P, S, "bank6", nc.vector.tensor_copy)
+        lone(7, 2 * P, 3 * P, "bank5", nc.scalar.copy)
+        lone(4, 3 * P, S, "bank3", nc.vector.tensor_copy)
+        lone(5, 2 * P, S, "bank4", nc.scalar.copy)
+        lone(6, 2 * P, S, "bank6", nc.vector.tensor_copy)
+        lone(7, 3 * P, S, "bank7", nc.scalar.copy)

@@ -182,39 +182,27 @@ def tile_picked_splice_none_p_kernel(tc, x_words, x_scales, w1, w2, w3, offs, ne
         for lo, hi in PIECES:
             nc.vector.quantize_mx(out=z_codes[:, lo:hi].bitcast(FP8X4), scales=z_scales[:, lo:hi], in_=z_grouped[:, lo * PACK : hi * PACK])
 
-        stores = ((0, 0, P), (1, 0, 2 * P), (2, 0, 2 * P), (3, 0, 2 * P), (0, P, S), (1, 2 * P, S), (2, 2 * P, S), (3, 2 * P, S))
+        stores = ((0, 0, 128), (1, 0, 128), (2, 0, 256), (3, 0, 256), (0, 128, 512), (1, 128, 512), (2, 256, 512), (3, 256, 512))
         results = [sb("result%d" % n, [P, hi - lo], F32) for n, (m, lo, hi) in enumerate(stores)]
 
-        def last_product(m, acc, lo, hi):
-            rows = slice(m * P, (m + 1) * P)
-            product(acc, (w3_codes[:, rows], w3_scales[:, rows]), (z_codes[:, lo:hi], z_scales[:, lo:hi]))
-
-        def empty(n, acc, lo, hi, copy):
+        def fill(n, lo, hi, width, bank, copy, complete):
             m, first, last = stores[n]
-            copy(results[n][:, lo - first : hi - first], acc[:])
-            if hi == last:
-                nc.sync.dma_start(out[m * P : (m + 1) * P, first:last], results[n][:])
-
-        def lone(n, lo, hi, bank, copy):
+            rows = slice(m * P, (m + 1) * P)
             acc = psum.tile([P, hi - lo], F32, name="acc%d_%d" % (n, lo), tag=bank)
-            last_product(stores[n][0], acc[:], lo, hi)
-            empty(n, acc, lo, hi, copy)
+            for at_column in range(lo, hi, width):
+                columns = slice(at_column, at_column + width)
+                product(acc[:, at_column - lo : at_column - lo + width], (w3_codes[:, rows], w3_scales[:, rows]), (z_codes[:, columns], z_scales[:, columns]))
+            copy(results[n][:, lo - first : hi - first], acc[:])
+            if complete:
+                nc.sync.dma_start(out[rows, first:last], results[n][:])
 
-        lone(0, 0, P, "bank6", nc.scalar.copy)
-        acc_1 = psum.tile([P, 2 * P], F32, name="acc_1", tag="bank7")
-        acc_2 = psum.tile([P, 2 * P], F32, name="acc_2", tag="bank0")
-        for lo in (0, P):
-            last_product(1, acc_1[:, lo : lo + P], lo, lo + P)
-            last_product(2, acc_2[:, lo : lo + P], lo, lo + P)
-        empty(1, acc_1, 0, 2 * P, nc.scalar.copy)
-        empty(2, acc_2, 0, 2 * P, nc.vector.tensor_copy)
-        lone(3, 0, 2 * P, "bank1", nc.scalar.copy)
-        acc_4 = psum.tile([P, 2 * P], F32, name="acc_4", tag="bank2")
-        last_product(0, acc_4[:, :P], P, 2 * P)
-        last_product(0, acc_4[:, P:], 2 * P, 3 * P)
-        empty(4, acc_4, P, 3 * P, nc.vector.tensor_copy)
-        lone(7, 2 * P, 3 * P, "bank5", nc.scalar.copy)
-        lone(4, 3 * P, S, "bank3", nc.vector.tensor_copy)
-        lone(5, 2 * P, S, "bank4", nc.scalar.copy)
-        lone(6, 2 * P, S, "bank6", nc.vector.tensor_copy)
-        lone(7, 3 * P, S, "bank7", nc.scalar.copy)
+        fill(0, 0, 128, 128, "bank6", nc.scalar.copy, True)
+        fill(1, 0, 128, 128, "bank7", nc.scalar.copy, True)
+        fill(2, 0, 256, 128, "bank0", nc.vector.tensor_copy, True)
+        fill(3, 0, 256, 256, "bank1", nc.scalar.copy, True)
+        fill(4, 128, 384, 128, "bank2", nc.vector.tensor_copy, False)
+        fill(5, 128, 256, 128, "bank5", nc.scalar.copy, False)
+        fill(4, 384, 512, 128, "bank3", nc.vector.tensor_copy, True)
+        fill(5, 256, 512, 256, "bank4", nc.scalar.copy, True)
+        fill(6, 256, 512, 256, "bank6", nc.vector.tensor_copy, True)
+        fill(7, 256, 512, 256, "bank7", nc.scalar.copy, True)

@@ -182,7 +182,7 @@ def tile_picked_splice_none_p_kernel(tc, x_words, x_scales, w1, w2, w3, offs, ne
         for lo, hi in PIECES:
             nc.vector.quantize_mx(out=z_codes[:, lo:hi].bitcast(FP8X4), scales=z_scales[:, lo:hi], in_=z_grouped[:, lo * PACK : hi * PACK])
 
-        stores = ((0, 0, 128), (1, 0, 128), (2, 0, 256), (3, 0, 256), (0, 128, 512), (1, 128, 512), (2, 256, 512), (3, 256, 512))
+        stores = ((0, 0, 128), (1, 0, 128), (2, 0, 256), (3, 0, 384), (0, 128, 512), (1, 128, 512), (2, 256, 512), (3, 384, 512))
         results = [sb("result%d" % n, [P, hi - lo], F32) for n, (m, lo, hi) in enumerate(stores)]
 
         def fill(n, lo, hi, width, bank, copy, complete):
@@ -199,10 +199,11 @@ def tile_picked_splice_none_p_kernel(tc, x_words, x_scales, w1, w2, w3, offs, ne
         fill(0, 0, 128, 128, "bank6", nc.scalar.copy, True)
         fill(1, 0, 128, 128, "bank7", nc.scalar.copy, True)
         fill(2, 0, 256, 128, "bank0", nc.vector.tensor_copy, True)
-        fill(3, 0, 256, 256, "bank1", nc.scalar.copy, True)
+        fill(3, 0, 256, 256, "bank1", nc.scalar.copy, False)
+        fill(3, 256, 384, 128, "bank5", nc.vector.tensor_copy, True)
         fill(4, 128, 384, 128, "bank2", nc.vector.tensor_copy, False)
-        fill(5, 128, 256, 128, "bank5", nc.scalar.copy, False)
-        fill(4, 384, 512, 128, "bank3", nc.vector.tensor_copy, True)
-        fill(5, 256, 512, 256, "bank4", nc.scalar.copy, True)
-        fill(6, 256, 512, 256, "bank6", nc.vector.tensor_copy, True)
-        fill(7, 256, 512, 256, "bank7", nc.scalar.copy, True)
+        fill(4, 384, 512, 128, "bank3", nc.scalar.copy, True)
+        fill(5, 128, 384, 256, "bank4", nc.scalar.copy, False)
+        fill(5, 384, 512, 128, "bank6", nc.vector.tensor_copy, True)
+        fill(6, 256, 512, 256, "bank7", nc.scalar.copy, True)
+        fill(7, 384, 512, 128, "bank0", nc.vector.tensor_copy, True)

from contextlib import ExitStack

import concourse.mybir as mybir

K, T, S, V, N, H = 512, 1024, 512, 256, 512, 512
FLOPS = 2 * K * H * (S + V) + 2 * H * N * S

F32 = mybir.dt.float32
BF16 = mybir.dt.bfloat16
I32 = mybir.dt.int32
U32 = mybir.dt.uint32
U16 = mybir.dt.uint16
U8 = mybir.dt.uint8
FP8X4 = mybir.dt.float8_e4m3fn_x4
MULT, ADD = mybir.AluOpType.mult, mybir.AluOpType.add

P = 128
PACK = 4
ORDER = (1, 3, 0, 2)
PIECES = ((0, 128), (128, 256), (256, 384), (384, 512))


def tile_picked_splice_none_p_kernel(tc, x_words, x_scales, w1, w2, w3, offs, new, at, out):
    nc = tc.nc
    with ExitStack() as ctx:
        held = ctx.enter_context(tc.tile_pool(name="held", bufs=1))
        reused = ctx.enter_context(tc.tile_pool(name="reused", bufs=1))
        psum = ctx.enter_context(tc.psum_pool(name="psum", bufs=1))

        def sb(name, shape, dtype, tag=None):
            if isinstance(tag, int):
                return reused.tile(shape, dtype, name=name, tag=name, align_bytes=64, offset=tag)
            return held.tile(shape, dtype, name=name, tag=tag or name, align_bytes=64)

        def gpsimd_copy(dst, src):
            nc.gpsimd.tensor_scalar(dst, src, 1.0, 0.0, op0=MULT, op1=ADD)

        offs_sb = held.tile([P, S // 16], U16, name="offs_sb")
        new_sb = held.tile([P, V // 16], U16, name="new_sb")
        at_sb = held.tile([P, V // 16], U16, name="at_sb")
        words = sb("words", [P, T], I32)
        scales = sb("scales", [P, T], U8)
        w1_raw = sb("w1_raw", [P, PACK, H], F32)
        w2_raw = sb("w2_raw", [P, PACK, H], F32)
        w3_raw = sb("w3_raw", [P, PACK, N], F32, 0)

        nc.vector.memset(scales[:].bitcast(I32), 0)
        nc.sync.dma_start(words[:], x_words[0].rearrange("p c r -> p (c r)").bitcast(I32))
        nc.sync.dma_start(offs_sb[:], offs)
        nc.sync.dma_start(new_sb[:], new)
        for r in range(4):
            nc.sync.dma_start(scales[r:P:32, :].bitcast(I32), x_scales[0, r:16:4, :].bitcast(I32))
        nc.sync.dma_start(w1_raw[:], w1.rearrange("(p j) c -> p j c", j=PACK))
        for j in (0, 2):
            nc.sync.dma_start(w2_raw[:, j : j + 2, :], w2.rearrange("(p j) c -> p j c", j=PACK)[:, j : j + 2, :])
        nc.sync.dma_start(at_sb[:], at)
        w3_rows = w3.rearrange("(g t u) n -> t g u n", t=PACK, u=4)
        for t in range(PACK):
            nc.sync.dma_start(w3_raw[:, t, :], w3_rows[t])

        old_words = sb("old_words", [P, S], U32)
        old_scales = sb("old_scales", [P, S], U8)
        new_words = sb("new_words", [P, V], U32)
        new_scales = sb("new_scales", [P, V], U8)
        nc.vector.tensor_copy(old_words[:], words[:].bitcast(U32).indirect(offs_sb[:]))
        nc.vector.tensor_copy(old_scales[:], scales[:].indirect(offs_sb[:]))
        nc.vector.tensor_copy(new_words[:], words[:].bitcast(U32).indirect(new_sb[:]))
        nc.vector.tensor_copy(new_scales[:], scales[:].indirect(new_sb[:]))

        def round_plane(copy, raw, t, name, tag=None):
            grouped = sb(name, [P, P * PACK], BF16, tag)
            walk = "g u j" if copy is gpsimd_copy else "g j u"
            copy(
                grouped[:].rearrange("p (g u j) -> p " + walk, u=4, j=PACK),
                raw[:].rearrange("p j (g t u) -> p t " + walk, t=PACK, u=4)[:, t],
            )
            return grouped

        def round_rows(copy, raw, t, grouped, j):
            copy(
                grouped[:].rearrange("p (g u j) -> p g j u", u=4, j=PACK)[:, :, j : j + 2, :],
                raw[:].rearrange("p j (g t u) -> p t g j u", t=PACK, u=4)[:, t, :, j : j + 2, :],
            )

        def quantize(grouped, name, tag=None):
            width = grouped.shape[1] // PACK
            codes = sb(name + "_codes", [P, width], U32, tag)
            code_scales = sb(name + "_scales", [P, width], U8)
            nc.vector.quantize_mx(out=codes[:].bitcast(FP8X4), scales=code_scales[:], in_=grouped)
            return codes, code_scales

        def product(acc, lhs, rhs):
            nc.tensor.matmul_mx(
                out=acc, lhsT=lhs[0].bitcast(FP8X4), lhsT_scale=lhs[1], rhs=rhs[0].bitcast(FP8X4), rhs_scale=rhs[1], start=True, stop=True
            )

        a, b, c, d = ORDER
        w1_grouped = {}
        for t, copy in ((a, gpsimd_copy), (b, nc.scalar.copy), (c, nc.scalar.copy), (d, gpsimd_copy)):
            w1_grouped[t] = round_plane(copy, w1_raw, t, "w1g%d" % t)
        w1_q = {t: quantize(w1_grouped[t][:], "w1q%d" % t, {c: 9216, d: 8192}.get(t)) for t in ORDER}

        y_acc, z, e = {}, {}, {}

        def old_product(t, bank):
            y_acc[t] = psum.tile([P, S], F32, name="y_acc%d" % t, tag=bank)
            product(y_acc[t][:], (w1_q[t][0][:], w1_q[t][1][:]), (old_words[:], old_scales[:]))

        def old_copy(t, width, tag=None):
            z[t] = sb("z%d" % t, [P, width], F32, tag)
            nc.scalar.copy(z[t][:, :S], y_acc[t][:])

        def new_product(t, acc, tag=None):
            codes, code_scales = quantize(w2_grouped[t][:], "w2q%d" % t, tag)
            product(acc, (codes[:], code_scales[:]), (new_words[:], new_scales[:]))

        def new_copy(planes, acc, tag=None):
            values = sb("e%d" % planes[0], [P, len(planes), V], F32, tag)
            nc.scalar.copy(values[:], acc[:])
            for i, t in enumerate(planes):
                e[t] = values[:, i, :]

        def scatter(t):
            nc.vector.tensor_copy(z[t][:].indirect(at_sb[:]), e[t])

        old_product(a, "bank0")
        old_product(b, "bank1")
        w2_grouped = {t: sb("w2g%d" % t, [P, P * PACK], BF16, tag) for t, tag in ((a, "w3g"), (b, None))}
        for t in (a, b):
            round_rows(nc.scalar.copy, w2_raw, t, w2_grouped[t], 0)
        for t in (a, b):
            round_rows(nc.vector.tensor_copy, w2_raw, t, w2_grouped[t], 2)
        w2_grouped[c] = round_plane(nc.scalar.copy, w2_raw, c, "w2g%d" % c)
        old_copy(a, S, "w1g%d" % d)
        e_acc_b = psum.tile([P, 1, V], F32, name="e_acc_b", tag="bank3")
        e_acc_cd = psum.tile([P, 2, V], F32, name="e_acc_cd", tag="bank4")
        codes, code_scales = quantize(w2_grouped[a][:], "w2q%d" % a)
        e_first = sb("e%d" % a, [P, V], F32)
        for lo, bank in ((0, "bank2"), (P, "bank5")):
            acc = psum.tile([P, P], F32, name="e_acc_a%d" % lo, tag=bank)
            product(acc[:], (codes[:], code_scales[:]), (new_words[:, lo : lo + P], new_scales[:, lo : lo + P]))
            nc.scalar.copy(e_first[:, lo : lo + P], acc[:])
        e[a] = e_first[:]
        new_product(b, e_acc_b[:, 0, :], "zb")
        w2_grouped[d] = round_plane(nc.vector.tensor_copy, w2_raw, d, "w2g%d" % d, "w3g")
        new_product(c, e_acc_cd[:, 0, :])
        new_product(d, e_acc_cd[:, 1, :])
        old_copy(b, S, "zb")
        new_copy((b,), e_acc_b)
        new_copy((c, d), e_acc_cd)
        old_product(c, "bank3")
        old_copy(c, 2 * S, 9216)
        old_product(d, "bank3")

        w3_grouped = sb("w3g", [P, N * PACK], BF16)
        gpsimd_copy(w3_grouped[:].rearrange("p (n t) -> p n t", t=PACK), w3_raw[:].rearrange("p t n -> p n t"))

        scatter(a)
        nc.scalar.copy(z[c][:, S:], z[a][:])
        old_copy(d, 2 * S, 4608)
        scatter(b)
        nc.scalar.copy(z[d][:, S:], z[b][:])
        scatter(c)

        z_grouped = sb("zg", [P, S * PACK], BF16, 0)

        def round_pair(copy, t, lo, hi):
            copy(
                z_grouped[:].rearrange("p (n t) -> p n t", t=PACK)[:, lo:hi, t : t + 2],
                z[t][:].rearrange("p (s n) -> p n s", s=2)[:, lo:hi, :],
            )

        round_pair(nc.scalar.copy, c, 0, 3 * P)
        round_pair(gpsimd_copy, c, 3 * P, S)
        scatter(d)
        w3_codes, w3_scales = quantize(w3_grouped[:], "w3q", 9216)
        for lo, hi in PIECES:
            round_pair(nc.scalar.copy, d, lo, hi)

        z_codes = sb("z_codes", [P, S], U32)
        z_scales = sb("z_scales", [P, S], U8)
        for lo, hi in PIECES:
            nc.vector.quantize_mx(out=z_codes[:, lo:hi].bitcast(FP8X4), scales=z_scales[:, lo:hi], in_=z_grouped[:, lo * PACK : hi * PACK])

        stores = ((0, 0, 128), (1, 0, 128), (2, 0, 256), (3, 0, 384), (0, 128, 512), (1, 128, 512), (2, 256, 512), (3, 384, 512))
        results = [sb("result%d" % n, [P, hi - lo], F32) for n, (m, lo, hi) in enumerate(stores)]

        def fill(n, lo, hi, width, bank, copy, complete):
            m, first, last = stores[n]
            rows = slice(m * P, (m + 1) * P)
            acc = psum.tile([P, hi - lo], F32, name="acc%d_%d" % (n, lo), tag=bank)
            for at_column in range(lo, hi, width):
                columns = slice(at_column, at_column + width)
                product(acc[:, at_column - lo : at_column - lo + width], (w3_codes[:, rows], w3_scales[:, rows]), (z_codes[:, columns], z_scales[:, columns]))
            copy(results[n][:, lo - first : hi - first], acc[:])
            if complete:
                nc.sync.dma_start(out[rows, first:last], results[n][:])

        fill(0, 0, 128, 128, "bank6", nc.scalar.copy, True)
        fill(1, 0, 128, 128, "bank7", nc.scalar.copy, True)
        fill(2, 0, 256, 128, "bank0", nc.vector.tensor_copy, True)
        fill(3, 0, 256, 256, "bank1", nc.scalar.copy, False)
        fill(3, 256, 384, 128, "bank5", nc.vector.tensor_copy, True)
        fill(4, 128, 384, 128, "bank2", nc.vector.tensor_copy, False)
        fill(4, 384, 512, 128, "bank3", nc.scalar.copy, True)
        fill(5, 128, 384, 256, "bank4", nc.scalar.copy, False)
        fill(5, 384, 512, 128, "bank6", nc.vector.tensor_copy, True)
        fill(6, 256, 512, 256, "bank7", nc.scalar.copy, True)
        fill(7, 384, 512, 128, "bank0", nc.vector.tensor_copy, True)
